import numpy as np
import ml_dtypes


def mxq(x, axis, fmt="e4m3"):
    dtype, down = {"e4m3": (ml_dtypes.float8_e4m3fn, 7), "e5m2": (ml_dtypes.float8_e5m2, 14)}[fmt]
    v = np.moveaxis(np.asarray(x, np.float32).astype(ml_dtypes.bfloat16).astype(np.float64), axis, -1)
    blocks = v.reshape(v.shape[:-1] + (-1, 32))
    amax = np.abs(blocks).max(-1, keepdims=True)
    byte = np.maximum(np.where(amax > 0, np.frexp(amax)[1] - 1 + 127, 0) - down, 1)
    scale = np.exp2(byte - 127.0)
    codes = (blocks / scale).astype(np.float32).astype(dtype).astype(np.float64)
    return np.moveaxis((codes * scale).reshape(v.shape), -1, axis)


WIDE = False


def mx_kscale(k):
    if not WIDE:
        return np.ones(k)
    levels = np.array([10, -10, 5, -5, 0])
    if k % 512:
        return np.exp2(np.random.permutation(np.resize(levels, k // 32))).repeat(32)
    a = np.empty((k // 512, 16))
    for p in range(k // 512):
        a[p, :8] = np.random.permutation(np.resize(levels, 8))
        for g in range(8):
            far = levels[np.abs(levels - a[p, g]) >= 10]
            a[p, g + 8] = far[np.random.randint(len(far))]
    return np.exp2(a.ravel()).repeat(32)


def f64(x):
    return np.asarray(x).astype(np.float64)


def striped(idx):
    return np.tile(idx.reshape(-1, 16).T, (8, 1)).astype(np.uint16)


def unstriped(offs):
    return offs[:16].T.reshape(-1).astype(np.int64)


def striped8(idx):
    return np.concatenate([x.reshape(-1, 16).T for x in idx]).astype(np.uint16)


def runs(offs, k):
    lists = np.stack([offs[16 * r : 16 * r + 16].T.reshape(-1) for r in range(8)]).astype(np.int64)
    return lists[np.arange(k) % 512 // 64]


def pack_weight(w):
    k, n = w.shape
    w = f64(np.asarray(w, np.float32).astype(ml_dtypes.bfloat16)).reshape(k // 32, 32, n)
    amax = np.abs(w).max(1)
    byte = np.clip(np.where(amax > 0, np.frexp(amax)[1] - 1 + 127 - 7, 1), 1, 254)
    scaled = (w * np.exp2(127.0 - byte)[:, None, :]).reshape(k, n).astype(np.float32)
    words = np.ascontiguousarray(scaled.reshape(k // 512, 128, 4, n).transpose(0, 1, 3, 2)).astype(ml_dtypes.float8_e4m3fn).view(np.uint8)
    return words, np.ascontiguousarray(byte.astype(np.uint8).reshape(k // 512, 16, n))


def unpack_weight(words, scales):
    g, p, n, _ = words.shape
    vals = np.ascontiguousarray(words).view(ml_dtypes.float8_e4m3fn).astype(np.float64) * np.repeat(np.exp2(scales.astype(np.float64) - 127.0), 8, axis=1)[..., None]
    return vals.transpose(0, 1, 3, 2).reshape(g * 512, n)


K, T, S, N, H, W = 512, 2048, 256, 512, 512, 192


def setup_inputs():
    n = np.random.standard_normal
    s = mx_kscale(K)[:, None]
    u = mx_kscale(H)
    packed_xT = pack_weight(n((K, T)) * s)
    return {
        "x_words": packed_xT[0],
        "x_scales": packed_xT[1],
        "w1": (n((K, H)) / np.sqrt(K) / s).astype(np.float32),
        "w2": (n((K, H)) / np.sqrt(K) / s).astype(np.float32),
        "gn": (np.random.uniform(0.5, 1.5, (H, 1)) * u[:, None]).astype(np.float32),
        "gm": (np.random.uniform(0.5, 1.5, (H, 1)) * u[:, None]).astype(np.float32),
        "w3": (n((H, N)) / np.sqrt(2 * H) / u[:, None]).astype(np.float32),
        "w4": (n((H, N)) / np.sqrt(2 * H) / u[:, None]).astype(np.float32),
        "offs": striped(np.random.permutation(T)[:S]),
        "hz": striped8(np.random.randint(0, T, (8, S))),
        "n1": striped(np.random.permutation(S)[:W]),
        "n2": striped(np.random.permutation(S)[:W]),
        "n3": striped(np.random.permutation(S)),
        "n4": striped(np.random.permutation(S)),
        "n5": striped(np.random.permutation(S)),
    }


def reference(x_words, x_scales, w1, w2, gn, gm, w3, w4, offs, hz, n1, n2, n3, n4, n5):
    xq = unpack_weight(x_words, x_scales)[:, unstriped(offs)]
    y = mxq(f64(w1), 0, "e4m3").T @ xq
    pa = y[:, unstriped(n2)]
    old = y[:, unstriped(n1)]
    ra = np.maximum(pa, 0.5 * old)
    ds = y.copy()
    ds[:, unstriped(n1)] = ra
    z = f64(gn) * ds
    x_hz = unpack_weight(x_words, x_scales)[np.arange(K)[:, None], runs(hz, K)]
    d = mxq(f64(w2), 0, "e4m3").T @ x_hz
    st = np.maximum(d, d[:, unstriped(n3)])
    z2 = f64(gm) * (np.minimum(st, st[:, unstriped(n4)]))
    h = mxq(f64(w3), 0, "e4m3").T @ mxq(z, 0, "e4m3") + mxq(f64(w4), 0, "e4m3").T @ mxq(z2, 0, "e4m3")
    return h - h[:, unstriped(n5)]

@@ -1,0 +1,214 @@
+from contextlib import ExitStack
+
+import concourse.mybir as mybir
+
+K, T, S, N, H, W = 512, 2048, 256, 512, 512, 192
+FLOPS = 4 * 2 * 512 * 512 * 256
+
+F32 = mybir.dt.float32
+BF16 = mybir.dt.bfloat16
+U32 = mybir.dt.uint32
+I32 = mybir.dt.int32
+U16 = mybir.dt.uint16
+U8 = mybir.dt.uint8
+FP8X4 = mybir.dt.float8_e4m3fn_x4
+ALU = mybir.AluOpType
+COPY = mybir.ActivationFunctionType.Copy
+
+P = 128
+PACK = 4
+SPARE = 8
+SC_W2 = 24
+SC_W1 = 0
+N4_ON_SCALAR = 2
+Y_OUT_ON_SCALAR = 2
+
+
+def tile_picked_hjoinkmaxhopmndif_none_p_kernel(tc, x_words, x_scales, w1, w2, gn, gm, w3, w4, offs, hz, n1, n2, n3, n4, n5, out):
+    nc = tc.nc
+    with ExitStack() as ctx:
+        lists = ctx.enter_context(tc.tile_pool(name="lists", bufs=1))
+        keep = ctx.enter_context(tc.tile_pool(name="keep", bufs=1))
+        stage = ctx.enter_context(tc.tile_pool(name="stage", bufs=1))
+        psum = ctx.enter_context(tc.psum_pool(name="psum", bufs=1))
+
+        def load_list(name, src, entries):
+            tile = lists.tile([P, entries // 16], U16, name=name)
+            nc.sync.dma_start(tile[:], src)
+            return tile
+
+        def load_weight(name, w, tag):
+            raw = stage.tile([P, PACK, w.shape[1]], F32, name=name, tag=tag, align_bytes=64)
+            nc.sync.dma_start(raw[:], w.rearrange("(p j) c -> p j c", j=PACK))
+            return raw
+
+        def load_gain(name, g):
+            tile = keep.tile([P, PACK], F32, name=name)
+            nc.gpsimd.dma_start(tile[:], g.rearrange("(p t) o -> p (t o)", t=PACK))
+            return tile
+
+        x_bytes = stage.tile([P, T], U8, name="x_bytes", tag="first", align_bytes=64)
+        nc.sync.dma_start(x_bytes[:].bitcast(I32), x_scales[0].bitcast(I32).unsqueeze(1).to_broadcast([16, 8, T // 4]))
+        hz_t = load_list("hz_t", hz, S)
+        offs_t = load_list("offs_t", offs, S)
+        n3_t = load_list("n3_t", n3, S)
+        n4_t = load_list("n4_t", n4, S)
+        n2_t = load_list("n2_t", n2, W)
+        n1_t = load_list("n1_t", n1, W)
+        x_codes = stage.tile([P, T], U32, name="x_codes", tag="codes", align_bytes=64)
+        nc.sync.dma_start(x_codes[:].bitcast(I32), x_words[0].rearrange("p n t -> p (n t)").bitcast(I32))
+        raw2 = [load_weight("raw2a", w2[:, 0:256], "second"), load_weight("raw2b", w2[:, 256:], "third")]
+        n5_t = load_list("n5_t", n5, S)
+        gm_t = load_gain("gm_t", gm)
+        gn_t = load_gain("gn_t", gn)
+
+        wide = [keep.tile([P, S + SPARE], F32, name=f"wide{t}") for t in range(PACK)]
+        for t in range(PACK):
+            nc.gpsimd.memset(wide[t][:, S:], 0.0)
+
+        gm_abs = keep.tile([P, PACK], F32, name="gm_abs")
+        nc.scalar.activation(gm_abs[:], gm_t[:], mybir.ActivationFunctionType.Abs)
+        gm_sign = keep.tile([P, 16, PACK], BF16, name="gm_sign", align_bytes=64)
+        nc.scalar.activation(gm_sign[:], gm_t[:].unsqueeze(1).to_broadcast([P, 16, PACK]), mybir.ActivationFunctionType.Sign)
+
+        picked_bytes = keep.tile([P, 2 * S], U8, name="picked_bytes", align_bytes=64)
+        nc.vector.tensor_copy(picked_bytes[:, 0:S], x_bytes[:].indirect(hz_t[:]))
+        nc.vector.tensor_copy(picked_bytes[:, S:], x_bytes[:].indirect(offs_t[:]))
+        plane = keep.tile([P, 2 * S], U8, name="plane", align_bytes=64)
+        nc.vector.memset(plane[:].bitcast(I32), 0)
+        for r in range(4):
+            nc.sync.dma_start(plane[:].bitcast(I32)[r:P:32, :], picked_bytes[:].bitcast(I32)[8 * r : P : 32, :])
+        raw1 = load_weight("raw1", w1, "first")
+
+        def quantize_dealt(name, raws, on_scalar):
+            grouped = keep.tile([P, 4 * 512], BF16, name=name + "_bf", align_bytes=64)
+            codes = keep.tile([P, 512], U32, name=name + "_codes", align_bytes=64)
+            scales = keep.tile([P, 512], U8, name=name + "_scales", align_bytes=64)
+            dealt = grouped[:].rearrange("p (t m j) -> p m j t", t=PACK, j=PACK)
+            span = P // len(raws)
+            for i, raw in enumerate(raws):
+                dst = dealt[:, span * i : span * (i + 1)]
+                src = raw[:].rearrange("p j (m t) -> p m j t", t=PACK)
+                split = span - (on_scalar if i == len(raws) - 1 else 0)
+                nc.vector.tensor_copy(dst[:, 0:split], src[:, 0:split])
+                if split < span:
+                    nc.scalar.activation(dst[:, split:], src[:, split:], COPY)
+            for t in range(PACK):
+                cols = slice(P * t, P * (t + 1))
+                nc.vector.quantize_mx(out=codes[:, cols].bitcast(FP8X4), scales=scales[:, cols], in_=grouped[:, 512 * t : 512 * (t + 1)])
+            return codes, scales
+
+        def round_plain(name, raw):
+            grouped = keep.tile([P, 4 * 512], BF16, name=name + "_bf", align_bytes=64)
+            nc.vector.tensor_copy(
+                grouped[:].rearrange("p (c i j) -> p c j i", i=4, j=PACK),
+                raw[:].rearrange("p j (c i) -> p c j i", i=4),
+            )
+            return grouped
+
+        def quantize(name, values, width):
+            codes = keep.tile([P, width], U32, name=name + "_codes", align_bytes=64)
+            scales = keep.tile([P, width], U8, name=name + "_scales", align_bytes=64)
+            nc.vector.quantize_mx(out=codes[:].bitcast(FP8X4), scales=scales[:], in_=values)
+            return codes, scales
+
+        def product(acc, weights, t, codes, scales, start, stop):
+            cols = slice(P * t, P * (t + 1))
+            nc.tensor.matmul_mx(
+                out=acc[:],
+                lhsT=weights[0][:, cols].bitcast(FP8X4),
+                lhsT_scale=weights[1][:, cols],
+                rhs=codes.bitcast(FP8X4),
+                rhs_scale=scales,
+                start=start,
+                stop=stop,
+            )
+
+        hashed = keep.tile([P, S], U32, name="hashed", align_bytes=64)
+        nc.vector.tensor_copy(hashed[:], x_codes[:].indirect(hz_t[:]))
+        picked = keep.tile([P, S], U32, name="picked", align_bytes=64)
+        nc.vector.tensor_copy(picked[:], x_codes[:].indirect(offs_t[:]))
+        q2 = quantize_dealt("w2", raw2, SC_W2)
+        d_acc = [psum.tile([P, S], F32, name=f"d_acc{t}", tag=f"bank{t}") for t in range(PACK)]
+        for t in range(PACK):
+            product(d_acc[t], q2, t, hashed[:], plane[:, 0:S], True, True)
+
+        q1 = quantize_dealt("w1", [raw1], SC_W1)
+        y_acc = [psum.tile([P, S], F32, name=f"y_acc{t}", tag=f"bank{PACK + t}") for t in range(PACK)]
+        for t in range(PACK):
+            product(y_acc[t], q1, t, picked[:], plane[:, S:], True, True)
+        raw3 = load_weight("raw3", w3, "second")
+        raw4 = load_weight("raw4", w4, "third")
+
+        st = keep.tile([P, PACK, 2 * S], F32, name="st")
+        st_far = keep.tile([P, PACK, S], F32, name="st_far")
+        for t in range(PACK):
+            nc.scalar.activation(wide[t][:, 0:S], d_acc[t][:], COPY, scale=gm_abs[:, t : t + 1])
+        for t in range(PACK):
+            nc.scalar.activation(st[:, t, S:], wide[t][:].indirect(n3_t[:]), COPY)
+            nc.vector.tensor_tensor(st[:, t, 0:S], wide[t][:, 0:S], st[:, t, S:], ALU.max)
+        for t in range(PACK):
+            if t < N4_ON_SCALAR:
+                nc.scalar.activation(st_far[:, t, :], st[:, t, :].indirect(n4_t[:]), COPY)
+            else:
+                nc.vector.tensor_copy(st_far[:, t, :], st[:, t, :].indirect(n4_t[:]))
+
+        y = [keep.tile([P, S], F32, name=f"y{t}") for t in range(PACK)]
+        for t in range(PACK):
+            if t < Y_OUT_ON_SCALAR:
+                nc.scalar.activation(y[t][:], y_acc[t][:], COPY)
+            else:
+                nc.vector.tensor_copy(y[t][:], y_acc[t][:])
+
+        pa = [keep.tile([P, W], F32, name=f"pa{t}") for t in range(PACK)]
+        old = [keep.tile([P, W], F32, name=f"old{t}") for t in range(PACK)]
+        for t in range(PACK):
+            nc.scalar.activation(pa[t][:], y[t][:].indirect(n2_t[:]), COPY)
+            nc.scalar.activation(old[t][:], y[t][:].indirect(n1_t[:]), COPY)
+
+        def larger(ra, first):
+            for i in range(2):
+                nc.vector.scalar_tensor_tensor(ra[:, i, :], old[first + i][:], 0.5, pa[first + i][:], ALU.mult, ALU.max)
+                nc.scalar.activation(y[first + i][:].indirect(n1_t[:]), ra[:, i, :], COPY)
+
+        w3_bf = round_plain("w3", raw3)
+        ra_early = stage.tile([P, 2, W], F32, name="ra_early", tag="second", align_bytes=64)
+        larger(ra_early, 0)
+        z2_size = stage.tile([P, S * PACK], BF16, name="z2_size", tag="size", align_bytes=64)
+        nc.vector.tensor_tensor(
+            z2_size[:].rearrange("p (c i t) -> p c t i", i=4, t=PACK),
+            st[:, :, 0:S].rearrange("p t (c i) -> p c t i", i=4),
+            st_far[:].rearrange("p t (c i) -> p c t i", i=4),
+            ALU.min,
+        )
+        q3 = quantize("w3", w3_bf[:], 512)
+        z2_bf = keep.tile([P, S * PACK], BF16, name="z2_bf", align_bytes=64)
+        nc.vector.tensor_tensor(
+            z2_bf[:].rearrange("p (a b) -> p a b", b=64),
+            z2_size[:].rearrange("p (a b) -> p a b", b=64),
+            gm_sign[:].rearrange("p a t -> p (a t)").unsqueeze(1).to_broadcast([P, 16, 64]),
+            ALU.mult,
+        )
+        w4_bf = round_plain("w4", raw4)
+        ra_late = stage.tile([P, 2, W], F32, name="ra_late", tag="size", align_bytes=64)
+        larger(ra_late, 2)
+        z2_codes, z2_scales = quantize("z2", z2_bf[:], S)
+        q4 = quantize("w4", w4_bf[:], 512)
+        z_bf = stage.tile([P, S, PACK], BF16, name="z_bf", tag="third", align_bytes=64)
+        for t in range(PACK):
+            nc.vector.tensor_scalar(z_bf[:, :, t], y[t][:], gn_t[:, t : t + 1], None, ALU.mult)
+        z_codes, z_scales = quantize("z", z_bf[:].rearrange("p j t -> p (j t)"), S)
+
+        h_acc = [psum.tile([P, S], F32, name=f"h_acc{t}", tag=f"bank{t}") for t in range(PACK)]
+        for t in range(PACK):
+            product(h_acc[t], q4, t, z2_codes[:], z2_scales[:], True, False)
+        for t in range(PACK):
+            product(h_acc[t], q3, t, z_codes[:], z_scales[:], False, True)
+        for t in range(PACK):
+            nc.vector.tensor_copy(wide[t][:, 0:S], h_acc[t][:])
+        for t in range(PACK):
+            h_far = keep.tile([P, S], F32, name=f"h_far{t}")
+            nc.scalar.activation(h_far[:], wide[t][:].indirect(n5_t[:]), COPY)
+            result = keep.tile([P, S], F32, name=f"result{t}")
+            nc.vector.tensor_tensor(result[:], wide[t][:, 0:S], h_far[:], ALU.subtract)
+            nc.sync.dma_start(out[P * t : P * (t + 1), :], result[:])

@@ -18,10 +18,11 @@ COPY = mybir.ActivationFunctionType.Copy
 P = 128
 PACK = 4
 SPARE = 8
-SC_W2 = 24
-SC_W1 = 0
-N4_ON_SCALAR = 2
-Y_OUT_ON_SCALAR = 2
+GP_W4 = 256
+SC_W2 = 0
+SC_W1 = 16
+N4_ON_SCALAR = 0
+Y_OUT_ON_SCALAR = 0
 
 
 def tile_picked_hjoinkmaxhopmndif_none_p_kernel(tc, x_words, x_scales, w1, w2, gn, gm, w3, w4, offs, hz, n1, n2, n3, n4, n5, out):
@@ -55,9 +56,9 @@ def tile_picked_hjoinkmaxhopmndif_none_p_kernel(tc, x_words, x_scales, w1, w2, g
         n4_t = load_list("n4_t", n4, S)
         n2_t = load_list("n2_t", n2, W)
         n1_t = load_list("n1_t", n1, W)
-        x_codes = stage.tile([P, T], U32, name="x_codes", tag="codes", align_bytes=64)
+        raw2 = load_weight("raw2", w2, "second")
+        x_codes = stage.tile([P, T], U32, name="x_codes", tag="third", align_bytes=64)
         nc.sync.dma_start(x_codes[:].bitcast(I32), x_words[0].rearrange("p n t -> p (n t)").bitcast(I32))
-        raw2 = [load_weight("raw2a", w2[:, 0:256], "second"), load_weight("raw2b", w2[:, 256:], "third")]
         n5_t = load_list("n5_t", n5, S)
         gm_t = load_gain("gm_t", gm)
         gn_t = load_gain("gn_t", gn)
@@ -78,33 +79,40 @@ def tile_picked_hjoinkmaxhopmndif_none_p_kernel(tc, x_words, x_scales, w1, w2, g
         nc.vector.memset(plane[:].bitcast(I32), 0)
         for r in range(4):
             nc.sync.dma_start(plane[:].bitcast(I32)[r:P:32, :], picked_bytes[:].bitcast(I32)[8 * r : P : 32, :])
-        raw1 = load_weight("raw1", w1, "first")
+        raw1 = stage.tile([P, 2, PACK, 256], F32, name="raw1", tag="first", align_bytes=64)
+        for half in range(2):
+            nc.sync.dma_start(raw1[:, half], w1[:, 256 * half : 256 * (half + 1)].rearrange("(p j) c -> p j c", j=PACK))
 
-        def quantize_dealt(name, raws, on_scalar):
-            grouped = keep.tile([P, 4 * 512], BF16, name=name + "_bf", align_bytes=64)
+        def quantize_dealt(name, raws, on_scalar, calls):
+            grouped = stage.tile([P, 4 * 512], BF16, name=name + "_bf", tag=name + "_bf", align_bytes=64)
             codes = keep.tile([P, 512], U32, name=name + "_codes", align_bytes=64)
             scales = keep.tile([P, 512], U8, name=name + "_scales", align_bytes=64)
             dealt = grouped[:].rearrange("p (t m j) -> p m j t", t=PACK, j=PACK)
             span = P // len(raws)
             for i, raw in enumerate(raws):
                 dst = dealt[:, span * i : span * (i + 1)]
-                src = raw[:].rearrange("p j (m t) -> p m j t", t=PACK)
+                src = raw.rearrange("p j (m t) -> p m j t", t=PACK)
                 split = span - (on_scalar if i == len(raws) - 1 else 0)
                 nc.vector.tensor_copy(dst[:, 0:split], src[:, 0:split])
                 if split < span:
                     nc.scalar.activation(dst[:, split:], src[:, split:], COPY)
-            for t in range(PACK):
-                cols = slice(P * t, P * (t + 1))
-                nc.vector.quantize_mx(out=codes[:, cols].bitcast(FP8X4), scales=scales[:, cols], in_=grouped[:, 512 * t : 512 * (t + 1)])
+            width = 512 // calls
+            for i in range(calls):
+                cols = slice(width * i, width * (i + 1))
+                nc.vector.quantize_mx(out=codes[:, cols].bitcast(FP8X4), scales=scales[:, cols], in_=grouped[:, 4 * width * i : 4 * width * (i + 1)])
             return codes, scales
 
-        def round_plain(name, raw):
-            grouped = keep.tile([P, 4 * 512], BF16, name=name + "_bf", align_bytes=64)
-            nc.vector.tensor_copy(
-                grouped[:].rearrange("p (c i j) -> p c j i", i=4, j=PACK),
-                raw[:].rearrange("p j (c i) -> p c j i", i=4),
-            )
-            return grouped
+        def round_plain(name, raw, tag, on_gpsimd):
+            grouped = stage.tile([P, 512, PACK], BF16, name=name + "_bf", tag=tag, align_bytes=64)
+            for first in range(0, on_gpsimd, 256):
+                cols = slice(first, first + 256)
+                nc.gpsimd.tensor_scalar(grouped[:, cols, :], raw[:, :, cols].rearrange("p j c -> p c j"), 1.0, 0.0, ALU.mult, ALU.add)
+            if on_gpsimd < 512:
+                nc.vector.tensor_copy(
+                    grouped[:, on_gpsimd:, :].rearrange("p (c i) j -> p c j i", i=4),
+                    raw[:, :, on_gpsimd:].rearrange("p j (c i) -> p c j i", i=4),
+                )
+            return grouped[:].rearrange("p c j -> p (c j)")
 
         def quantize(name, values, width):
             codes = keep.tile([P, width], U32, name=name + "_codes", align_bytes=64)
@@ -115,7 +123,7 @@ def tile_picked_hjoinkmaxhopmndif_none_p_kernel(tc, x_words, x_scales, w1, w2, g
         def product(acc, weights, t, codes, scales, start, stop):
             cols = slice(P * t, P * (t + 1))
             nc.tensor.matmul_mx(
-                out=acc[:],
+                out=acc,
                 lhsT=weights[0][:, cols].bitcast(FP8X4),
                 lhsT_scale=weights[1][:, cols],
                 rhs=codes.bitcast(FP8X4),
@@ -124,64 +132,66 @@ def tile_picked_hjoinkmaxhopmndif_none_p_kernel(tc, x_words, x_scales, w1, w2, g
                 stop=stop,
             )
 
+        q2 = quantize_dealt("w2", [raw2[:]], SC_W2, 1)
         hashed = keep.tile([P, S], U32, name="hashed", align_bytes=64)
         nc.vector.tensor_copy(hashed[:], x_codes[:].indirect(hz_t[:]))
-        picked = keep.tile([P, S], U32, name="picked", align_bytes=64)
-        nc.vector.tensor_copy(picked[:], x_codes[:].indirect(offs_t[:]))
-        q2 = quantize_dealt("w2", raw2, SC_W2)
         d_acc = [psum.tile([P, S], F32, name=f"d_acc{t}", tag=f"bank{t}") for t in range(PACK)]
         for t in range(PACK):
-            product(d_acc[t], q2, t, hashed[:], plane[:, 0:S], True, True)
+            product(d_acc[t][:], q2, t, hashed[:], plane[:, 0:S], True, True)
+        picked = keep.tile([P, S], U32, name="picked", align_bytes=64)
+        nc.vector.tensor_copy(picked[:], x_codes[:].indirect(offs_t[:]))
 
-        q1 = quantize_dealt("w1", [raw1], SC_W1)
+        q1 = quantize_dealt("w1", [raw1[:, 0], raw1[:, 1]], SC_W1, 2)
         y_acc = [psum.tile([P, S], F32, name=f"y_acc{t}", tag=f"bank{PACK + t}") for t in range(PACK)]
         for t in range(PACK):
-            product(y_acc[t], q1, t, picked[:], plane[:, S:], True, True)
+            product(y_acc[t][:], q1, t, picked[:], plane[:, S:], True, True)
         raw3 = load_weight("raw3", w3, "second")
         raw4 = load_weight("raw4", w4, "third")
 
-        st = keep.tile([P, PACK, 2 * S], F32, name="st")
-        st_far = keep.tile([P, PACK, S], F32, name="st_far")
+        st = stage.tile([P, PACK, 2 * S], F32, name="st", tag="first", align_bytes=64)
+        st_far = stage.tile([P, PACK, S], F32, name="st_far", tag="far", align_bytes=64)
+        y = [keep.tile([P, S], F32, name=f"y{t}") for t in range(PACK)]
         for t in range(PACK):
             nc.scalar.activation(wide[t][:, 0:S], d_acc[t][:], COPY, scale=gm_abs[:, t : t + 1])
         for t in range(PACK):
             nc.scalar.activation(st[:, t, S:], wide[t][:].indirect(n3_t[:]), COPY)
-            nc.vector.tensor_tensor(st[:, t, 0:S], wide[t][:, 0:S], st[:, t, S:], ALU.max)
+            nc.vector.scalar_tensor_tensor(st[:, t, 0:S], d_acc[t][:], gm_abs[:, t : t + 1], st[:, t, S:], ALU.mult, ALU.max)
+            if t < PACK - Y_OUT_ON_SCALAR:
+                nc.vector.tensor_copy(y[t][:], y_acc[t][:])
         for t in range(PACK):
             if t < N4_ON_SCALAR:
                 nc.scalar.activation(st_far[:, t, :], st[:, t, :].indirect(n4_t[:]), COPY)
             else:
                 nc.vector.tensor_copy(st_far[:, t, :], st[:, t, :].indirect(n4_t[:]))
 
-        y = [keep.tile([P, S], F32, name=f"y{t}") for t in range(PACK)]
+
+        pa = [keep.tile([P, 2, W], F32, name=f"pa{i}") for i in range(2)]
+        old = [keep.tile([P, 2, W], F32, name=f"old{i}") for i in range(2)]
         for t in range(PACK):
-            if t < Y_OUT_ON_SCALAR:
+            if t >= PACK - Y_OUT_ON_SCALAR:
                 nc.scalar.activation(y[t][:], y_acc[t][:], COPY)
-            else:
-                nc.vector.tensor_copy(y[t][:], y_acc[t][:])
+            nc.scalar.activation(pa[t // 2][:, t % 2, :], y[t][:].indirect(n2_t[:]), COPY)
+            nc.scalar.activation(old[t // 2][:, t % 2, :], y[t][:].indirect(n1_t[:]), COPY)
 
-        pa = [keep.tile([P, W], F32, name=f"pa{t}") for t in range(PACK)]
-        old = [keep.tile([P, W], F32, name=f"old{t}") for t in range(PACK)]
-        for t in range(PACK):
-            nc.scalar.activation(pa[t][:], y[t][:].indirect(n2_t[:]), COPY)
-            nc.scalar.activation(old[t][:], y[t][:].indirect(n1_t[:]), COPY)
-
-        def larger(ra, first):
+        def larger(ra, pair):
+            nc.vector.scalar_tensor_tensor(ra[:], old[pair][:], 0.5, pa[pair][:], ALU.mult, ALU.max)
             for i in range(2):
-                nc.vector.scalar_tensor_tensor(ra[:, i, :], old[first + i][:], 0.5, pa[first + i][:], ALU.mult, ALU.max)
-                nc.scalar.activation(y[first + i][:].indirect(n1_t[:]), ra[:, i, :], COPY)
+                nc.scalar.activation(y[2 * pair + i][:].indirect(n1_t[:]), ra[:, i, :], COPY)
 
-        w3_bf = round_plain("w3", raw3)
-        ra_early = stage.tile([P, 2, W], F32, name="ra_early", tag="second", align_bytes=64)
+        w3_bf = round_plain("w3", raw3, "w1_bf", 512)
+        ra_early = keep.tile([P, 2, W], F32, name="ra_early")
         larger(ra_early, 0)
-        z2_size = stage.tile([P, S * PACK], BF16, name="z2_size", tag="size", align_bytes=64)
+        w4_bf = round_plain("w4", raw4, "w2_bf", GP_W4)
+        z2_size = keep.tile([P, S * PACK], BF16, name="z2_size", align_bytes=64)
         nc.vector.tensor_tensor(
             z2_size[:].rearrange("p (c i t) -> p c t i", i=4, t=PACK),
             st[:, :, 0:S].rearrange("p t (c i) -> p c t i", i=4),
             st_far[:].rearrange("p t (c i) -> p c t i", i=4),
             ALU.min,
         )
-        q3 = quantize("w3", w3_bf[:], 512)
+        q3 = quantize("w3", w3_bf, 512)
+        ra_late = stage.tile([P, 2, W], F32, name="ra_late", tag="far", align_bytes=64)
+        larger(ra_late, 1)
         z2_bf = keep.tile([P, S * PACK], BF16, name="z2_bf", align_bytes=64)
         nc.vector.tensor_tensor(
             z2_bf[:].rearrange("p (a b) -> p a b", b=64),
@@ -189,26 +199,28 @@ def tile_picked_hjoinkmaxhopmndif_none_p_kernel(tc, x_words, x_scales, w1, w2, g
             gm_sign[:].rearrange("p a t -> p (a t)").unsqueeze(1).to_broadcast([P, 16, 64]),
             ALU.mult,
         )
-        w4_bf = round_plain("w4", raw4)
-        ra_late = stage.tile([P, 2, W], F32, name="ra_late", tag="size", align_bytes=64)
-        larger(ra_late, 2)
         z2_codes, z2_scales = quantize("z2", z2_bf[:], S)
-        q4 = quantize("w4", w4_bf[:], 512)
+        q4 = quantize("w4", w4_bf, 512)
         z_bf = stage.tile([P, S, PACK], BF16, name="z_bf", tag="third", align_bytes=64)
-        for t in range(PACK):
+        halves = [slice(0, S // 2), slice(S // 2, S)]
+        for t in range(PACK - 1):
             nc.vector.tensor_scalar(z_bf[:, :, t], y[t][:], gn_t[:, t : t + 1], None, ALU.mult)
-        z_codes, z_scales = quantize("z", z_bf[:].rearrange("p j t -> p (j t)"), S)
+        for cols in halves:
+            nc.vector.tensor_scalar(z_bf[:, cols, PACK - 1], y[PACK - 1][:, cols], gn_t[:, PACK - 1 :], None, ALU.mult)
+        qz = [quantize(f"z{i}", z_bf[:, cols, :].rearrange("p j t -> p (j t)"), S // 2) for i, cols in enumerate(halves)]
 
         h_acc = [psum.tile([P, S], F32, name=f"h_acc{t}", tag=f"bank{t}") for t in range(PACK)]
         for t in range(PACK):
-            product(h_acc[t], q4, t, z2_codes[:], z2_scales[:], True, False)
+            product(h_acc[t][:], q4, t, z2_codes[:], z2_scales[:], True, False)
         for t in range(PACK):
-            product(h_acc[t], q3, t, z_codes[:], z_scales[:], False, True)
+            for i, cols in enumerate(halves):
+                product(h_acc[t][:, cols], q3, t, qz[i][0][:], qz[i][1][:], False, i == 1)
         for t in range(PACK):
             nc.vector.tensor_copy(wide[t][:, 0:S], h_acc[t][:])
         for t in range(PACK):
             h_far = keep.tile([P, S], F32, name=f"h_far{t}")
-            nc.scalar.activation(h_far[:], wide[t][:].indirect(n5_t[:]), COPY)
             result = keep.tile([P, S], F32, name=f"result{t}")
-            nc.vector.tensor_tensor(result[:], wide[t][:, 0:S], h_far[:], ALU.subtract)
-            nc.sync.dma_start(out[P * t : P * (t + 1), :], result[:])
+            for cols in halves if t == PACK - 1 else [slice(0, S)]:
+                nc.scalar.activation(h_far[:, cols], wide[t][:].indirect(n5_t[:, cols.start // 16 : cols.stop // 16]), COPY)
+                nc.vector.tensor_tensor(result[:, cols], wide[t][:, cols], h_far[:, cols], ALU.subtract)
+                nc.sync.dma_start(out[P * t : P * (t + 1), cols], result[:, cols])

@@ -20,8 +20,8 @@ PACK = 4
 SPARE = 8
 GP_W4 = 256
 SC_W2 = 0
-SC_W1 = 16
-N4_ON_SCALAR = 0
+SC_W1 = 0
+N4_ON_SCALAR = 1
 Y_OUT_ON_SCALAR = 0
 
 
@@ -148,21 +148,23 @@ def tile_picked_hjoinkmaxhopmndif_none_p_kernel(tc, x_words, x_scales, w1, w2, g
         raw3 = load_weight("raw3", w3, "second")
         raw4 = load_weight("raw4", w4, "third")
 
-        st = stage.tile([P, PACK, 2 * S], F32, name="st", tag="first", align_bytes=64)
+        st = stage.tile([P, (PACK + 1) * S], F32, name="st", tag="first", align_bytes=64)
+        d_early = keep.tile([P, (PACK - 1) * S], F32, name="d_early")
+        d_far = [d_early[:, S * t : S * (t + 1)] for t in range(PACK - 1)] + [st[:, PACK * S :]]
         st_far = stage.tile([P, PACK, S], F32, name="st_far", tag="far", align_bytes=64)
         y = [keep.tile([P, S], F32, name=f"y{t}") for t in range(PACK)]
         for t in range(PACK):
             nc.scalar.activation(wide[t][:, 0:S], d_acc[t][:], COPY, scale=gm_abs[:, t : t + 1])
         for t in range(PACK):
-            nc.scalar.activation(st[:, t, S:], wide[t][:].indirect(n3_t[:]), COPY)
-            nc.vector.scalar_tensor_tensor(st[:, t, 0:S], d_acc[t][:], gm_abs[:, t : t + 1], st[:, t, S:], ALU.mult, ALU.max)
+            nc.scalar.activation(d_far[t], wide[t][:].indirect(n3_t[:]), COPY)
+            nc.vector.scalar_tensor_tensor(st[:, S * t : S * (t + 1)], d_acc[t][:], gm_abs[:, t : t + 1], d_far[t], ALU.mult, ALU.max)
             if t < PACK - Y_OUT_ON_SCALAR:
                 nc.vector.tensor_copy(y[t][:], y_acc[t][:])
         for t in range(PACK):
             if t < N4_ON_SCALAR:
-                nc.scalar.activation(st_far[:, t, :], st[:, t, :].indirect(n4_t[:]), COPY)
+                nc.scalar.activation(st_far[:, t, :], st[:, S * t : S * (t + 2)].indirect(n4_t[:]), COPY)
             else:
-                nc.vector.tensor_copy(st_far[:, t, :], st[:, t, :].indirect(n4_t[:]))
+                nc.vector.tensor_copy(st_far[:, t, :], st[:, S * t : S * (t + 2)].indirect(n4_t[:]))
 
 
         pa = [keep.tile([P, 2, W], F32, name=f"pa{i}") for i in range(2)]
@@ -185,7 +187,7 @@ def tile_picked_hjoinkmaxhopmndif_none_p_kernel(tc, x_words, x_scales, w1, w2, g
         z2_size = keep.tile([P, S * PACK], BF16, name="z2_size", align_bytes=64)
         nc.vector.tensor_tensor(
             z2_size[:].rearrange("p (c i t) -> p c t i", i=4, t=PACK),
-            st[:, :, 0:S].rearrange("p t (c i) -> p c t i", i=4),
+            st[:, 0 : PACK * S].rearrange("p (t c i) -> p c t i", t=PACK, i=4),
             st_far[:].rearrange("p t (c i) -> p c t i", i=4),
             ALU.min,
         )
@@ -203,8 +205,10 @@ def tile_picked_hjoinkmaxhopmndif_none_p_kernel(tc, x_words, x_scales, w1, w2, g
         q4 = quantize("w4", w4_bf, 512)
         z_bf = stage.tile([P, S, PACK], BF16, name="z_bf", tag="third", align_bytes=64)
         halves = [slice(0, S // 2), slice(S // 2, S)]
+        z_rows = keep.tile([P, PACK - 1, S], BF16, name="z_rows", align_bytes=64)
         for t in range(PACK - 1):
-            nc.vector.tensor_scalar(z_bf[:, :, t], y[t][:], gn_t[:, t : t + 1], None, ALU.mult)
+            nc.vector.tensor_scalar(z_rows[:, t, :], y[t][:], gn_t[:, t : t + 1], None, ALU.mult)
+        nc.vector.tensor_copy(z_bf[:, :, 0 : PACK - 1], z_rows[:].rearrange("p t j -> p j t"))
         for cols in halves:
             nc.vector.tensor_scalar(z_bf[:, cols, PACK - 1], y[PACK - 1][:, cols], gn_t[:, PACK - 1 :], None, ALU.mult)
         qz = [quantize(f"z{i}", z_bf[:, cols, :].rearrange("p j t -> p (j t)"), S // 2) for i, cols in enumerate(halves)]

from contextlib import ExitStack

import concourse.mybir as mybir

K, T, S, N, H, W = 512, 2048, 256, 512, 512, 192
FLOPS = 4 * 2 * 512 * 512 * 256

F32 = mybir.dt.float32
BF16 = mybir.dt.bfloat16
U32 = mybir.dt.uint32
I32 = mybir.dt.int32
U16 = mybir.dt.uint16
U8 = mybir.dt.uint8
FP8X4 = mybir.dt.float8_e4m3fn_x4
ALU = mybir.AluOpType
COPY = mybir.ActivationFunctionType.Copy

P = 128
PACK = 4
SPARE = 8
GP_W4 = 256
SC_W2 = 0
SC_W1 = 0
N4_ON_SCALAR = 1
Y_OUT_ON_SCALAR = 0


def tile_picked_hjoinkmaxhopmndif_none_p_kernel(tc, x_words, x_scales, w1, w2, gn, gm, w3, w4, offs, hz, n1, n2, n3, n4, n5, out):
    nc = tc.nc
    with ExitStack() as ctx:
        lists = ctx.enter_context(tc.tile_pool(name="lists", bufs=1))
        keep = ctx.enter_context(tc.tile_pool(name="keep", bufs=1))
        stage = ctx.enter_context(tc.tile_pool(name="stage", bufs=1))
        psum = ctx.enter_context(tc.psum_pool(name="psum", bufs=1))

        def load_list(name, src, entries):
            tile = lists.tile([P, entries // 16], U16, name=name)
            nc.sync.dma_start(tile[:], src)
            return tile

        def load_weight(name, w, tag):
            raw = stage.tile([P, PACK, w.shape[1]], F32, name=name, tag=tag, align_bytes=64)
            nc.sync.dma_start(raw[:], w.rearrange("(p j) c -> p j c", j=PACK))
            return raw

        def load_gain(name, g):
            tile = keep.tile([P, PACK], F32, name=name)
            nc.gpsimd.dma_start(tile[:], g.rearrange("(p t) o -> p (t o)", t=PACK))
            return tile

        x_bytes = stage.tile([P, T], U8, name="x_bytes", tag="first", align_bytes=64)
        nc.sync.dma_start(x_bytes[:].bitcast(I32), x_scales[0].bitcast(I32).unsqueeze(1).to_broadcast([16, 8, T // 4]))
        hz_t = load_list("hz_t", hz, S)
        offs_t = load_list("offs_t", offs, S)
        n3_t = load_list("n3_t", n3, S)
        n4_t = load_list("n4_t", n4, S)
        n2_t = load_list("n2_t", n2, W)
        n1_t = load_list("n1_t", n1, W)
        raw2 = load_weight("raw2", w2, "second")
        x_codes = stage.tile([P, T], U32, name="x_codes", tag="third", align_bytes=64)
        nc.sync.dma_start(x_codes[:].bitcast(I32), x_words[0].rearrange("p n t -> p (n t)").bitcast(I32))
        n5_t = load_list("n5_t", n5, S)
        gm_t = load_gain("gm_t", gm)
        gn_t = load_gain("gn_t", gn)

        wide = [keep.tile([P, S + SPARE], F32, name=f"wide{t}") for t in range(PACK)]
        for t in range(PACK):
            nc.gpsimd.memset(wide[t][:, S:], 0.0)

        gm_abs = keep.tile([P, PACK], F32, name="gm_abs")
        nc.scalar.activation(gm_abs[:], gm_t[:], mybir.ActivationFunctionType.Abs)
        gm_sign = keep.tile([P, 16, PACK], BF16, name="gm_sign", align_bytes=64)
        nc.scalar.activation(gm_sign[:], gm_t[:].unsqueeze(1).to_broadcast([P, 16, PACK]), mybir.ActivationFunctionType.Sign)

        picked_bytes = keep.tile([P, 2 * S], U8, name="picked_bytes", align_bytes=64)
        nc.vector.tensor_copy(picked_bytes[:, 0:S], x_bytes[:].indirect(hz_t[:]))
        nc.vector.tensor_copy(picked_bytes[:, S:], x_bytes[:].indirect(offs_t[:]))
        plane = keep.tile([P, 2 * S], U8, name="plane", align_bytes=64)
        nc.vector.memset(plane[:].bitcast(I32), 0)
        for r in range(4):
            nc.sync.dma_start(plane[:].bitcast(I32)[r:P:32, :], picked_bytes[:].bitcast(I32)[8 * r : P : 32, :])
        raw1 = stage.tile([P, 2, PACK, 256], F32, name="raw1", tag="first", align_bytes=64)
        for half in range(2):
            nc.sync.dma_start(raw1[:, half], w1[:, 256 * half : 256 * (half + 1)].rearrange("(p j) c -> p j c", j=PACK))

        def quantize_dealt(name, raws, on_scalar, calls):
            grouped = stage.tile([P, 4 * 512], BF16, name=name + "_bf", tag=name + "_bf", align_bytes=64)
            codes = keep.tile([P, 512], U32, name=name + "_codes", align_bytes=64)
            scales = keep.tile([P, 512], U8, name=name + "_scales", align_bytes=64)
            dealt = grouped[:].rearrange("p (t m j) -> p m j t", t=PACK, j=PACK)
            span = P // len(raws)
            for i, raw in enumerate(raws):
                dst = dealt[:, span * i : span * (i + 1)]
                src = raw.rearrange("p j (m t) -> p m j t", t=PACK)
                split = span - (on_scalar if i == len(raws) - 1 else 0)
                nc.vector.tensor_copy(dst[:, 0:split], src[:, 0:split])
                if split < span:
                    nc.scalar.activation(dst[:, split:], src[:, split:], COPY)
            width = 512 // calls
            for i in range(calls):
                cols = slice(width * i, width * (i + 1))
                nc.vector.quantize_mx(out=codes[:, cols].bitcast(FP8X4), scales=scales[:, cols], in_=grouped[:, 4 * width * i : 4 * width * (i + 1)])
            return codes, scales

        def round_plain(name, raw, tag, on_gpsimd):
            grouped = stage.tile([P, 512, PACK], BF16, name=name + "_bf", tag=tag, align_bytes=64)
            for first in range(0, on_gpsimd, 256):
                cols = slice(first, first + 256)
                nc.gpsimd.tensor_scalar(grouped[:, cols, :], raw[:, :, cols].rearrange("p j c -> p c j"), 1.0, 0.0, ALU.mult, ALU.add)
            if on_gpsimd < 512:
                nc.vector.tensor_copy(
                    grouped[:, on_gpsimd:, :].rearrange("p (c i) j -> p c j i", i=4),
                    raw[:, :, on_gpsimd:].rearrange("p j (c i) -> p c j i", i=4),
                )
            return grouped[:].rearrange("p c j -> p (c j)")

        def quantize(name, values, width):
            codes = keep.tile([P, width], U32, name=name + "_codes", align_bytes=64)
            scales = keep.tile([P, width], U8, name=name + "_scales", align_bytes=64)
            nc.vector.quantize_mx(out=codes[:].bitcast(FP8X4), scales=scales[:], in_=values)
            return codes, scales

        def product(acc, weights, t, codes, scales, start, stop):
            cols = slice(P * t, P * (t + 1))
            nc.tensor.matmul_mx(
                out=acc,
                lhsT=weights[0][:, cols].bitcast(FP8X4),
                lhsT_scale=weights[1][:, cols],
                rhs=codes.bitcast(FP8X4),
                rhs_scale=scales,
                start=start,
                stop=stop,
            )

        q2 = quantize_dealt("w2", [raw2[:]], SC_W2, 1)
        hashed = keep.tile([P, S], U32, name="hashed", align_bytes=64)
        nc.vector.tensor_copy(hashed[:], x_codes[:].indirect(hz_t[:]))
        d_acc = [psum.tile([P, S], F32, name=f"d_acc{t}", tag=f"bank{t}") for t in range(PACK)]
        for t in range(PACK):
            product(d_acc[t][:], q2, t, hashed[:], plane[:, 0:S], True, True)
        picked = keep.tile([P, S], U32, name="picked", align_bytes=64)
        nc.vector.tensor_copy(picked[:], x_codes[:].indirect(offs_t[:]))

        q1 = quantize_dealt("w1", [raw1[:, 0], raw1[:, 1]], SC_W1, 2)
        y_acc = [psum.tile([P, S], F32, name=f"y_acc{t}", tag=f"bank{PACK + t}") for t in range(PACK)]
        for t in range(PACK):
            product(y_acc[t][:], q1, t, picked[:], plane[:, S:], True, True)
        raw3 = load_weight("raw3", w3, "second")
        raw4 = load_weight("raw4", w4, "third")

        st = stage.tile([P, (PACK + 1) * S], F32, name="st", tag="first", align_bytes=64)
        d_early = keep.tile([P, (PACK - 1) * S], F32, name="d_early")
        d_far = [d_early[:, S * t : S * (t + 1)] for t in range(PACK - 1)] + [st[:, PACK * S :]]
        st_far = stage.tile([P, PACK, S], F32, name="st_far", tag="far", align_bytes=64)
        y = [keep.tile([P, S], F32, name=f"y{t}") for t in range(PACK)]
        for t in range(PACK):
            nc.scalar.activation(wide[t][:, 0:S], d_acc[t][:], COPY, scale=gm_abs[:, t : t + 1])
        for t in range(PACK):
            nc.scalar.activation(d_far[t], wide[t][:].indirect(n3_t[:]), COPY)
            nc.vector.scalar_tensor_tensor(st[:, S * t : S * (t + 1)], d_acc[t][:], gm_abs[:, t : t + 1], d_far[t], ALU.mult, ALU.max)
            if t < PACK - Y_OUT_ON_SCALAR:
                nc.vector.tensor_copy(y[t][:], y_acc[t][:])
        for t in range(PACK):
            if t < N4_ON_SCALAR:
                nc.scalar.activation(st_far[:, t, :], st[:, S * t : S * (t + 2)].indirect(n4_t[:]), COPY)
            else:
                nc.vector.tensor_copy(st_far[:, t, :], st[:, S * t : S * (t + 2)].indirect(n4_t[:]))


        pa = [keep.tile([P, 2, W], F32, name=f"pa{i}") for i in range(2)]
        old = [keep.tile([P, 2, W], F32, name=f"old{i}") for i in range(2)]
        for t in range(PACK):
            if t >= PACK - Y_OUT_ON_SCALAR:
                nc.scalar.activation(y[t][:], y_acc[t][:], COPY)
            nc.scalar.activation(pa[t // 2][:, t % 2, :], y[t][:].indirect(n2_t[:]), COPY)
            nc.scalar.activation(old[t // 2][:, t % 2, :], y[t][:].indirect(n1_t[:]), COPY)

        def larger(ra, pair):
            nc.vector.scalar_tensor_tensor(ra[:], old[pair][:], 0.5, pa[pair][:], ALU.mult, ALU.max)
            for i in range(2):
                nc.scalar.activation(y[2 * pair + i][:].indirect(n1_t[:]), ra[:, i, :], COPY)

        w3_bf = round_plain("w3", raw3, "w1_bf", 512)
        ra_early = keep.tile([P, 2, W], F32, name="ra_early")
        larger(ra_early, 0)
        w4_bf = round_plain("w4", raw4, "w2_bf", GP_W4)
        z2_size = keep.tile([P, S * PACK], BF16, name="z2_size", align_bytes=64)
        nc.vector.tensor_tensor(
            z2_size[:].rearrange("p (c i t) -> p c t i", i=4, t=PACK),
            st[:, 0 : PACK * S].rearrange("p (t c i) -> p c t i", t=PACK, i=4),
            st_far[:].rearrange("p t (c i) -> p c t i", i=4),
            ALU.min,
        )
        q3 = quantize("w3", w3_bf, 512)
        ra_late = stage.tile([P, 2, W], F32, name="ra_late", tag="far", align_bytes=64)
        larger(ra_late, 1)
        z2_bf = keep.tile([P, S * PACK], BF16, name="z2_bf", align_bytes=64)
        nc.vector.tensor_tensor(
            z2_bf[:].rearrange("p (a b) -> p a b", b=64),
            z2_size[:].rearrange("p (a b) -> p a b", b=64),
            gm_sign[:].rearrange("p a t -> p (a t)").unsqueeze(1).to_broadcast([P, 16, 64]),
            ALU.mult,
        )
        z2_codes, z2_scales = quantize("z2", z2_bf[:], S)
        q4 = quantize("w4", w4_bf, 512)
        z_bf = stage.tile([P, S, PACK], BF16, name="z_bf", tag="third", align_bytes=64)
        halves = [slice(0, S // 2), slice(S // 2, S)]
        z_rows = keep.tile([P, PACK - 1, S], BF16, name="z_rows", align_bytes=64)
        for t in range(PACK - 1):
            nc.vector.tensor_scalar(z_rows[:, t, :], y[t][:], gn_t[:, t : t + 1], None, ALU.mult)
        nc.vector.tensor_copy(z_bf[:, :, 0 : PACK - 1], z_rows[:].rearrange("p t j -> p j t"))
        for cols in halves:
            nc.vector.tensor_scalar(z_bf[:, cols, PACK - 1], y[PACK - 1][:, cols], gn_t[:, PACK - 1 :], None, ALU.mult)
        qz = [quantize(f"z{i}", z_bf[:, cols, :].rearrange("p j t -> p (j t)"), S // 2) for i, cols in enumerate(halves)]

        h_acc = [psum.tile([P, S], F32, name=f"h_acc{t}", tag=f"bank{t}") for t in range(PACK)]
        for t in range(PACK):
            product(h_acc[t][:], q4, t, z2_codes[:], z2_scales[:], True, False)
        for t in range(PACK):
            for i, cols in enumerate(halves):
                product(h_acc[t][:, cols], q3, t, qz[i][0][:], qz[i][1][:], False, i == 1)
        for t in range(PACK):
            nc.vector.tensor_copy(wide[t][:, 0:S], h_acc[t][:])
        for t in range(PACK):
            h_far = keep.tile([P, S], F32, name=f"h_far{t}")
            result = keep.tile([P, S], F32, name=f"result{t}")
            for cols in halves if t == PACK - 1 else [slice(0, S)]:
                nc.scalar.activation(h_far[:, cols], wide[t][:].indirect(n5_t[:, cols.start // 16 : cols.stop // 16]), COPY)
                nc.vector.tensor_tensor(result[:, cols], wide[t][:, cols], h_far[:, cols], ALU.subtract)
                nc.sync.dma_start(out[P * t : P * (t + 1), cols], result[:, cols])
